import numpy as np, ml_dtypes
CORES = [36,164,52,180,100,228,116,244]
N = 8
import mx_ref
NC, ROOT = 512, 5
BF = ml_dtypes.bfloat16
def cut(t, i, w=512):
    return t[:, w * i:w * i + w]
def term(a, B):
    return np.stack([np.maximum(mx_ref.matmul(mx_ref.quantize(cut(a, i)), B), 0) for i in range(4)], axis=2).reshape(128, -1)
def setup_inputs(rng):
    def f(*shape):
        return mx_ref.flush((rng.standard_normal(shape, dtype=np.float32) * np.exp2(rng.integers(-2, 3, shape[:-1] + (1,)))).astype(BF))
    return {"a": f(N, 128, 4 * 512), "b": f(N, 128, 4 * NC)}
def setup_inputs_blocks(rng):
    d = setup_inputs(rng)
    for k in ("a", "b"): d[k] = mx_ref.spread(d[k], rng, 2)
    return d
def setup_inputs_wide(rng):
    d = setup_inputs(rng)
    for k in ("a", "b"): d[k] = mx_ref.flush((d[k].astype(np.float32) * np.exp2(rng.integers(-4, 5, (N, 1, 1))).astype(np.float32)).astype(BF))
    return d
def setup_inputs_lossless(rng):
    a = np.zeros((N, 128, 4 * 128, 4), np.float32)
    for r in range(N):
        k = rng.integers(0, 512, size=4 * 128)
        a[r, k // 4, np.arange(4 * 128), k % 4] = 1.0
    size = np.repeat(2.0 ** rng.integers(-4, 5, size=(1, 1, (4 * NC) // 4)), 4, axis=2)
    b = (rng.random((N, 128, 4 * NC)) < 0.8) * size
    return {"a": a.reshape(N, 128, 4 * 512).astype(BF), "b": b.astype(np.float32).astype(BF)}
def reference(a, b):
    B0 = mx_ref.quantize(b[ROOT])
    T = [term(a[r], B0) for r in range(N)]
    y = np.zeros((N, 128, 4 * NC), np.float32)
    y[:] = mx_ref.total(T)
    return {"y": y}

@@ -1,0 +1,267 @@
+from concourse.mybir import dt, AluOpType, ActivationFunctionType
+
+W = 128
+NC = 512
+CODE, BF, F32 = "float8_e4m3fn_x4", "bfloat16", "float32"
+
+SCRATCH = {
+    "abf": ("sbuf", [128, 2048], BF),
+    "qa": ("sbuf", [128, NC], CODE), "sa": ("sbuf", [128, NC], "uint8"),
+    "bbf": ("sbuf", [128, 2048], BF),
+    "qb": ("sbuf", [128, NC], CODE), "sb": ("sbuf", [128, NC], "uint8"),
+    "lb": ("sbuf", [128, W], CODE), "lbs": ("sbuf", [128, W], "uint8"),
+    "la1": ("sbuf", [128, NC], CODE), "las1": ("sbuf", [128, NC], "uint8"),
+    "la2": ("sbuf", [128, NC], CODE), "las2": ("sbuf", [128, NC], "uint8"),
+    "la3": ("sbuf", [128, NC], CODE), "las3": ("sbuf", [128, NC], "uint8"),
+    "t5": ("sbuf", [128, 2048], BF),
+    "qt": ("sbuf", [128, NC], CODE), "st": ("sbuf", [128, NC], "uint8"),
+    "lt": ("sbuf", [128, W], CODE), "lts": ("sbuf", [128, W], "uint8"),
+    "ones": ("sbuf", [128, W], BF), "dg": ("sbuf", [128, W], BF),
+    "cst": ("sbuf", [128, 4096], BF),
+    "qc": ("sbuf", [128, 2 * NC], CODE), "sc": ("sbuf", [128, 2 * NC], "uint8"),
+    "r0": ("sbuf", [128, NC], BF), "r1": ("sbuf", [128, NC], BF),
+    "r2": ("sbuf", [128, NC], BF), "r3": ("sbuf", [128, NC], BF),
+    "u1": ("sbuf", [128, NC], BF), "u2": ("sbuf", [128, NC], BF),
+    "p": ("sbuf", [128, NC], BF),
+    "qp": ("sbuf", [128, W], CODE), "sp": ("sbuf", [128, W], "uint8"),
+    "lp": ("sbuf", [128, W], CODE), "lps": ("sbuf", [128, W], "uint8"),
+    "tt": ("sbuf", [128, NC], BF),
+    "gq": ("sbuf", [128, NC], CODE), "gs": ("sbuf", [128, NC], "uint8"),
+    "ysb": ("sbuf", [128, 2048], F32),
+    "ps": ("psum", [128, 4096], F32),
+}
+SEMAPHORES = ["ld_b0", "ld_b1", "ld_a", "yst", "pe", "act", "dve", "gp", "loc",
+              "rB", "rA1", "rA2", "rA3", "rT", "rP", "rG1", "rG2", "rG3"]
+
+
+def rank_program(g, core, T, topo):
+    cores = T.cores
+    root = cores[T.root]
+    rank = T.rank_of(core)
+
+    near = [c for c in range(max(cores) + 8) if c < 256 and c not in cores
+            and topo.host(c) == topo.host(root) and topo.chip(c) == topo.chip(root)]
+    far_die = [c for c in near if topo.die(c) != topo.die(root)]
+    own_die = [c for c in near if topo.die(c) == topo.die(root)]
+    helper = [far_die[0], own_die[0], far_die[1]]
+    rq, rg = T.root // 2, T.root % 2
+    foreign = [q for q in range(4) if q != rq]
+    helper_of = {q: helper[i] for i, q in enumerate(foreign)}
+
+    sent, arrive = [0], {}
+
+    def engines(src, dst):
+        return bin(topo.mask(src, dst)).count("1")
+
+    def send(dst, out_q, in_q, out_s, in_s, sem):
+        rid, pid = topo.addr(dst, core)
+        m = topo.mask(core, dst)
+        g.remote_dma(out_q.bitcast(dt.uint8), in_q.bitcast(dt.uint8), T.sem[sem], T.sem.loc, pid, rid, m)
+        g.remote_dma(out_s, in_s, T.sem[sem], T.sem.loc, pid, rid, m)
+        sent[0] += 2 * engines(core, dst)
+
+    if rank is None:
+        for q in foreign:
+            if helper_of[q] == core:
+                g.wait_ge(T.sem.rB, 2 * engines(root, core))
+                for grp in (rg, 1 - rg):
+                    send(cores[2 * q + grp], T.lb[:, 0:W], T.lb[:, 0:W], T.lbs[:, 0:W], T.lbs[:, 0:W], "rB")
+                g.wait_ge(T.sem.loc, sent[0])
+        return
+
+    q, grp = rank // 2, rank % 2
+    is_root = core == root
+    with_term = grp == rg and not is_root
+    partner = cores[2 * q + 1 - grp]
+
+    def mate(k):
+        return cores[2 * ((q + k) % 4) + grp]
+
+    eng = {"pe": g.tensor, "act": g.scalar, "dve": g.vector, "gp": g, "sync": g.sync}
+    cnt = {"pe": 0, "act": 0, "dve": 0, "gp": 0}
+    seen = {}
+
+    def wait(queue, sem, n):
+        if seen.get((queue, sem), 0) < n:
+            seen[(queue, sem)] = n
+            eng[queue].wait_ge(T.sem[sem], n)
+
+    def did(queue, ins):
+        cnt[queue] += 1
+        ins.then_inc(T.sem[queue], 1)
+        return (queue, cnt[queue])
+
+    def need(queue, *ops):
+        for op in ops:
+            if op is not None:
+                wait(queue, op[0], op[1])
+
+    reader = {}
+
+    def bank(b, lo=0, hi=NC):
+        return T.ps[:, NC * b + lo:NC * b + hi]
+
+    def mm(b, lq, ls, rq_, rs, n, *deps):
+        need("pe", *deps)
+        need("pe", *reader.get(b, []))
+        reader[b] = []
+        return did("pe", g.tensor.matmul_mx(bank(b, 0, n), lq, ls, rq_, rs, True, True))
+
+    def relu(queue, out, b, lo, hi, *deps):
+        need(queue, *deps)
+        if queue == "act":
+            op = did(queue, g.scalar.activation(out, bank(b, lo, hi), ActivationFunctionType.Relu))
+        else:
+            op = did(queue, g.vector.tensor_scalar(out, bank(b, lo, hi), 0.0, None, AluOpType.max))
+        reader[b] = reader.get(b, []) + [op]
+        return op
+
+    def quant(oq, os, src, *deps):
+        need("dve", *deps)
+        return did("dve", g.vector.quantize_mx(oq, os, src))
+
+    def add(out, a, b, *deps, psum=None):
+        need("dve", *deps)
+        op = did("dve", g.vector.tensor_tensor(out, a, b, AluOpType.add))
+        if psum is not None:
+            reader[psum] = reader.get(psum, []) + [op]
+        return op
+
+    if is_root:
+        g.sync.dma_start(T.bbf[:, 0:1024], T.b[:, 0:1024]).then_inc(T.sem.ld_b0, 16)
+        g.sync.dma_start(T.bbf[:, 1024:2048], T.b[:, 1024:2048]).then_inc(T.sem.ld_b1, 16)
+        g.sync.wait_ge(T.sem.ld_b0, 16)
+    g.sync.dma_start(T.abf[:], T.a[:]).then_inc(T.sem.ld_a, 16)
+
+    ones = did("dve", g.vector.memset(T.ones[:], 1.0))
+    qb = {}
+    if is_root:
+        wait("dve", "ld_b0", 16)
+        h0 = quant(T.qb[:, 0:256], T.sb[:, 0:256], T.bbf[:, 0:1024])
+        wait("dve", "ld_b1", 16)
+        h1 = quant(T.qb[:, 256:512], T.sb[:, 256:512], T.bbf[:, 1024:2048])
+        qb = {0: h0, 1: h0, 2: h1, 3: h1}
+    z0 = did("dve", g.vector.memset(T.cst[:, 0:2048], 0.0))
+    z1 = did("dve", g.vector.memset(T.cst[:, 2048:4096], 0.0))
+    wait("dve", "ld_a", 16)
+    qa = quant(T.qa[:], T.sa[:], T.abf[:])
+
+    def make_diagonal():
+        need("gp", ones)
+        return did("gp", g.affine_select(T.dg[:], T.ones[:], [[-1, W]], AluOpType.is_equal, 0.0, 0, 1))
+
+    def spread_diagonal(diag):
+        need("act", diag, z0, z1)
+        cp = ActivationFunctionType.Copy
+        for i in range(4):
+            c0 = did("act", g.scalar.activation(T.cst[:, NC * i + i:NC * i + NC:4], T.dg[:], cp))
+        for t in range(4):
+            c1 = did("act", g.scalar.activation(T.cst[:, 2048 + 5 * t:4096:16], T.dg[:], cp))
+        return c0, c1
+
+    def quant_constants(c0, c1):
+        s = quant(T.qc[:, 0:NC], T.sc[:, 0:NC], T.cst[:, 0:2048], c0)
+        i = quant(T.qc[:, NC:2 * NC], T.sc[:, NC:2 * NC], T.cst[:, 2048:4096], c1)
+        return s, i
+
+    terms = []
+    if is_root:
+        for f in foreign:
+            need("gp", qb[f])
+            v = slice(W * f, W * f + W)
+            send(helper_of[f], T.lb[:, 0:W], T.qb[:, v], T.lbs[:, 0:W], T.sb[:, v], "rB")
+        v = slice(W * q, W * q + W)
+        need("gp", qb[q])
+        send(partner, T.lb[:, 0:W], T.qb[:, v], T.lbs[:, 0:W], T.sb[:, v], "rB")
+        diag = make_diagonal()
+        order = [(q + k) % 4 for k in (1, 2, 3)]
+        ready = {}
+        for n, f in enumerate(order + [q]):
+            v = slice(W * f, W * f + W)
+            z = mm(n, T.qb[:, v], T.sb[:, v], T.qa[:], T.sa[:], NC, qb[f], qa)
+            if f == q:
+                terms.append((relu("act", T.r0[:], n, 0, NC, z), T.r0))
+            else:
+                on = "dve" if n == 1 else "act"
+                ready[f] = [relu(on, T.t5[:, NC * f + i:NC * f + NC:4], n, W * i, W * i + W, z) for i in range(4)]
+        for f in order:
+            v = slice(W * f, W * f + W)
+            op = quant(T.qt[:, v], T.st[:, v], T.t5[:, NC * f:NC * f + NC], *ready[f])
+            need("gp", op)
+            send(cores[2 * f + grp], T.lt[:, 0:W], T.qt[:, v], T.lts[:, 0:W], T.st[:, v], "rT")
+        sel, idn = quant_constants(*spread_diagonal(diag))
+        bq, bs = T.qb[:, W * q:W * q + W], T.sb[:, W * q:W * q + W]
+        zbank = {1: 4, 2: 5, 3: 6}
+    else:
+        diag = make_diagonal()
+        need("gp", qa)
+        for k in (1, 2, 3):
+            send(mate(k), T["la%d" % k][:], T.qa[:], T["las%d" % k][:], T.sa[:], "rA%d" % k)
+        sel, idn = quant_constants(*spread_diagonal(diag))
+        bq, bs = T.lb[:, 0:W], T.lbs[:, 0:W]
+        src = helper_of[q] if q != rq else root
+        wait("pe", "rB", 2 * engines(src, core))
+        z = mm(0, bq, bs, T.qa[:], T.sa[:], NC, qa)
+        terms.append((relu("act", T.r0[:], 0, 0, NC, z), T.r0))
+        zbank = {1: 1, 2: 2, 3: 3}
+
+    for k in (1, 2, 3):
+        sender = mate(-k)
+        if sender == root:
+            continue
+        wait("pe", "rA%d" % k, 2 * engines(sender, core))
+        z = mm(zbank[k], bq, bs, T["la%d" % k][:], T["las%d" % k][:], NC)
+        buf = T["r%d" % k]
+        terms.append((relu("act", buf[:], zbank[k], 0, NC, z), buf))
+
+    op, acc = terms[0]
+    last = len(terms) - (0 if with_term else 1)
+    for n in range(1, last):
+        out = (T.u1, T.u2)[n % 2]
+        op = add(out[:], acc[:], terms[n][1][:], op, terms[n][0])
+        acc = out
+    ops = []
+    if with_term:
+        wait("pe", "rT", 2 * engines(root, core))
+        us = [mm(4 + i, T.qc[:, W * i:W * i + W], T.sc[:, W * i:W * i + W], T.lt[:, 0:W], T.lts[:, 0:W], W, sel)
+              for i in range(4)]
+        for i in range(4):
+            ops.append(add(T.p[:, i:NC:4], bank(4 + i, 0, W), acc[:, W * i:W * i + W], us[i], op, psum=4 + i))
+    else:
+        for i in range(4):
+            ops.append(add(T.p[:, i:NC:4], acc[:, W * i:W * i + W], terms[-1][1][:, W * i:W * i + W], op, terms[-1][0]))
+    op = quant(T.qp[:], T.sp[:], T.p[:], ops[-1])
+    need("gp", op)
+    send(partner, T.lp[:, 0:W], T.qp[:, 0:W], T.lps[:, 0:W], T.sp[:, 0:W], "rP")
+
+    vb = 0 if is_root else 4
+    wait("pe", "rP", 2 * engines(partner, core))
+    us = [mm(vb + i, T.qc[:, W * i:W * i + W], T.sc[:, W * i:W * i + W], T.lp[:, 0:W], T.lps[:, 0:W], W, sel)
+          for i in range(4)]
+    for i in range(4):
+        op = add(T.tt[:, i:NC:4], bank(vb + i, 0, W), T.p[:, i:NC:4], us[i], psum=vb + i)
+    v = slice(W * q, W * q + W)
+    tot = quant(T.gq[:, v], T.gs[:, v], T.tt[:], op)
+    need("gp", tot)
+    for k in (1, 2, 3):
+        send(mate(k), T.gq[:, v], T.gq[:, v], T.gs[:, v], T.gs[:, v], "rG%d" % k)
+
+    stored = 0
+    for k in range(4):
+        f = (q - k) % 4
+        v = slice(W * f, W * f + W)
+        if k:
+            wait("pe", "rG%d" % k, 2 * engines(mate(-k), core))
+        m = [mm(2 * k + h, T.gq[:, v], T.gs[:, v], T.qc[:, NC + 256 * h:NC + 256 * h + 256],
+                T.sc[:, NC + 256 * h:NC + 256 * h + 256], 256, idn, tot) for h in range(2)]
+        need("act", m[0])
+        c0 = did("act", g.scalar.activation(T.ysb[:, NC * f:NC * f + 256], bank(2 * k, 0, 256), ActivationFunctionType.Copy))
+        need("dve", m[1])
+        c1 = did("dve", g.vector.tensor_copy(T.ysb[:, NC * f + 256:NC * f + NC], bank(2 * k + 1, 0, 256)))
+        need("sync", c0, c1)
+        g.sync.dma_start(T.y[:, NC * f:NC * f + NC], T.ysb[:, NC * f:NC * f + NC]).then_inc(T.sem.yst, 16)
+        stored += 16
+    g.sync.wait_ge(T.sem.yst, stored)
+    g.wait_ge(T.sem.loc, sent[0])
+    for name in ("pe", "act", "dve", "gp"):
+        wait("sync", name, cnt[name])

@@ -2,6 +2,7 @@ from concourse.mybir import dt, AluOpType, ActivationFunctionType
 
 W = 128
 NC = 512
+H = 192
 CODE, BF, F32 = "float8_e4m3fn_x4", "bfloat16", "float32"
 
 SCRATCH = {
@@ -19,9 +20,10 @@ SCRATCH = {
     "ones": ("sbuf", [128, W], BF), "dg": ("sbuf", [128, W], BF),
     "cst": ("sbuf", [128, 4096], BF),
     "qc": ("sbuf", [128, 2 * NC], CODE), "sc": ("sbuf", [128, 2 * NC], "uint8"),
-    "r0": ("sbuf", [128, NC], BF), "r1": ("sbuf", [128, NC], BF),
-    "r2": ("sbuf", [128, NC], BF), "r3": ("sbuf", [128, NC], BF),
-    "u1": ("sbuf", [128, NC], BF), "u2": ("sbuf", [128, NC], BF),
+    "r0": ("sbuf", [128, NC], BF), "r1": ("sbuf", [128, NC], BF), "r2": ("sbuf", [128, NC], BF),
+    "u1": ("sbuf", [128, NC], BF),
+    "acc": ("sbuf", [128, NC], BF),
+    "qs": ("sbuf", [128, W], CODE), "ss": ("sbuf", [128, W], "uint8"),
     "p": ("sbuf", [128, NC], BF),
     "qp": ("sbuf", [128, W], CODE), "sp": ("sbuf", [128, W], "uint8"),
     "lp": ("sbuf", [128, W], CODE), "lps": ("sbuf", [128, W], "uint8"),
@@ -30,8 +32,8 @@ SCRATCH = {
     "ysb": ("sbuf", [128, 2048], F32),
     "ps": ("psum", [128, 4096], F32),
 }
-SEMAPHORES = ["ld_b0", "ld_b1", "ld_a", "yst", "pe", "act", "dve", "gp", "loc",
-              "rB", "rA1", "rA2", "rA3", "rT", "rP", "rG1", "rG2", "rG3"]
+SEMAPHORES = ["ld_b0", "ld_b1", "ld_a0", "ld_a1", "yst", "pe", "act", "dve", "gp", "loc",
+              "rH", "rB", "rA1", "rA2", "rA3", "rT", "rP", "rG1", "rG2", "rG3"]
 
 
 def rank_program(g, core, T, topo):
@@ -39,16 +41,16 @@ def rank_program(g, core, T, topo):
     root = cores[T.root]
     rank = T.rank_of(core)
 
-    near = [c for c in range(max(cores) + 8) if c < 256 and c not in cores
-            and topo.host(c) == topo.host(root) and topo.chip(c) == topo.chip(root)]
-    far_die = [c for c in near if topo.die(c) != topo.die(root)]
-    own_die = [c for c in near if topo.die(c) == topo.die(root)]
-    helper = [far_die[0], own_die[0], far_die[1]]
+    def far_cores(c):
+        return [d for d in range(max(cores) + 8) if d < 256 and d not in cores and topo.host(d) == topo.host(c)
+                and topo.chip(d) == topo.chip(c) and topo.die(d) != topo.die(c)]
+
     rq, rg = T.root // 2, T.root % 2
     foreign = [q for q in range(4) if q != rq]
-    helper_of = {q: helper[i] for i, q in enumerate(foreign)}
+    helper_of = {q: far_cores(root)[i] for i, q in enumerate(foreign)}
+    relay_of = {c: far_cores(c)[0] for c in cores if c != root}
 
-    sent, arrive = [0], {}
+    sent = [0]
 
     def engines(src, dst):
         return bin(topo.mask(src, dst)).count("1")
@@ -60,13 +62,24 @@ def rank_program(g, core, T, topo):
         g.remote_dma(out_s, in_s, T.sem[sem], T.sem.loc, pid, rid, m)
         sent[0] += 2 * engines(core, dst)
 
+    def send_a(owner, lo, hi):
+        r = T.rank_of(owner)
+        for k in (1, 2, 3):
+            send(cores[2 * ((r // 2 + k) % 4) + r % 2], T["la%d" % k][:, lo:hi], T.qa[:, lo:hi],
+                 T["las%d" % k][:, lo:hi], T.sa[:, lo:hi], "rA%d" % k)
+
     if rank is None:
         for q in foreign:
             if helper_of[q] == core:
                 g.wait_ge(T.sem.rB, 2 * engines(root, core))
                 for grp in (rg, 1 - rg):
                     send(cores[2 * q + grp], T.lb[:, 0:W], T.lb[:, 0:W], T.lbs[:, 0:W], T.lbs[:, 0:W], "rB")
-                g.wait_ge(T.sem.loc, sent[0])
+        for c in relay_of:
+            if relay_of[c] == core:
+                g.wait_ge(T.sem.rH, 2 * engines(c, core))
+                send_a(c, 0, H)
+        if sent[0]:
+            g.wait_ge(T.sem.loc, sent[0])
         return
 
     q, grp = rank // 2, rank % 2
@@ -101,11 +114,11 @@ def rank_program(g, core, T, topo):
     def bank(b, lo=0, hi=NC):
         return T.ps[:, NC * b + lo:NC * b + hi]
 
-    def mm(b, lq, ls, rq_, rs, n, *deps):
+    def mm(b, lq, ls, rq_, rs, n, *deps, start=True, stop=True):
         need("pe", *deps)
         need("pe", *reader.get(b, []))
         reader[b] = []
-        return did("pe", g.tensor.matmul_mx(bank(b, 0, n), lq, ls, rq_, rs, True, True))
+        return did("pe", g.tensor.matmul_mx(bank(b, 0, n), lq, ls, rq_, rs, start, stop))
 
     def relu(queue, out, b, lo, hi, *deps):
         need(queue, *deps)
@@ -120,9 +133,9 @@ def rank_program(g, core, T, topo):
         need("dve", *deps)
         return did("dve", g.vector.quantize_mx(oq, os, src))
 
-    def add(out, a, b, *deps, psum=None):
+    def two(out, a, b, alu, *deps, psum=None):
         need("dve", *deps)
-        op = did("dve", g.vector.tensor_tensor(out, a, b, AluOpType.add))
+        op = did("dve", g.vector.tensor_tensor(out, a, b, alu))
         if psum is not None:
             reader[psum] = reader.get(psum, []) + [op]
         return op
@@ -131,41 +144,40 @@ def rank_program(g, core, T, topo):
         g.sync.dma_start(T.bbf[:, 0:1024], T.b[:, 0:1024]).then_inc(T.sem.ld_b0, 16)
         g.sync.dma_start(T.bbf[:, 1024:2048], T.b[:, 1024:2048]).then_inc(T.sem.ld_b1, 16)
         g.sync.wait_ge(T.sem.ld_b0, 16)
-    g.sync.dma_start(T.abf[:], T.a[:]).then_inc(T.sem.ld_a, 16)
+        g.sync.dma_start(T.abf[:], T.a[:]).then_inc(T.sem.ld_a0, 16)
+    else:
+        g.sync.dma_start(T.abf[:, 0:4 * H], T.a[:, 0:4 * H]).then_inc(T.sem.ld_a0, 16)
+        g.sync.dma_start(T.abf[:, 4 * H:2048], T.a[:, 4 * H:2048]).then_inc(T.sem.ld_a1, 16)
 
     ones = did("dve", g.vector.memset(T.ones[:], 1.0))
-    qb = {}
-    if is_root:
-        wait("dve", "ld_b0", 16)
-        h0 = quant(T.qb[:, 0:256], T.sb[:, 0:256], T.bbf[:, 0:1024])
-        wait("dve", "ld_b1", 16)
-        h1 = quant(T.qb[:, 256:512], T.sb[:, 256:512], T.bbf[:, 1024:2048])
-        qb = {0: h0, 1: h0, 2: h1, 3: h1}
-    z0 = did("dve", g.vector.memset(T.cst[:, 0:2048], 0.0))
-    z1 = did("dve", g.vector.memset(T.cst[:, 2048:4096], 0.0))
-    wait("dve", "ld_a", 16)
-    qa = quant(T.qa[:], T.sa[:], T.abf[:])
 
     def make_diagonal():
         need("gp", ones)
         return did("gp", g.affine_select(T.dg[:], T.ones[:], [[-1, W]], AluOpType.is_equal, 0.0, 0, 1))
 
-    def spread_diagonal(diag):
-        need("act", diag, z0, z1)
+    def constants(diag):
+        z0 = did("dve", g.vector.memset(T.cst[:, 0:2048], 0.0))
+        z1 = did("dve", g.vector.memset(T.cst[:, 2048:4096], 0.0))
         cp = ActivationFunctionType.Copy
+        need("act", diag, z0)
         for i in range(4):
             c0 = did("act", g.scalar.activation(T.cst[:, NC * i + i:NC * i + NC:4], T.dg[:], cp))
+        need("act", z1)
         for t in range(4):
             c1 = did("act", g.scalar.activation(T.cst[:, 2048 + 5 * t:4096:16], T.dg[:], cp))
-        return c0, c1
-
-    def quant_constants(c0, c1):
         s = quant(T.qc[:, 0:NC], T.sc[:, 0:NC], T.cst[:, 0:2048], c0)
         i = quant(T.qc[:, NC:2 * NC], T.sc[:, NC:2 * NC], T.cst[:, 2048:4096], c1)
         return s, i
 
     terms = []
     if is_root:
+        wait("dve", "ld_b0", 16)
+        h0 = quant(T.qb[:, 0:256], T.sb[:, 0:256], T.bbf[:, 0:1024])
+        wait("dve", "ld_b1", 16)
+        h1 = quant(T.qb[:, 256:512], T.sb[:, 256:512], T.bbf[:, 1024:2048])
+        qb = {0: h0, 1: h0, 2: h1, 3: h1}
+        wait("dve", "ld_a0", 16)
+        qa = quant(T.qa[:], T.sa[:], T.abf[:])
         for f in foreign:
             need("gp", qb[f])
             v = slice(W * f, W * f + W)
@@ -189,57 +201,69 @@ def rank_program(g, core, T, topo):
             op = quant(T.qt[:, v], T.st[:, v], T.t5[:, NC * f:NC * f + NC], *ready[f])
             need("gp", op)
             send(cores[2 * f + grp], T.lt[:, 0:W], T.qt[:, v], T.lts[:, 0:W], T.st[:, v], "rT")
-        sel, idn = quant_constants(*spread_diagonal(diag))
+        sel, idn = constants(diag)
         bq, bs = T.qb[:, W * q:W * q + W], T.sb[:, W * q:W * q + W]
-        zbank = {1: 4, 2: 5, 3: 6}
+        zbank, lbank, vbank = {1: 4, 2: 5, 3: 6}, 0, 4
     else:
         diag = make_diagonal()
+        wait("dve", "ld_a0", 16)
+        qa0 = quant(T.qa[:, 0:H], T.sa[:, 0:H], T.abf[:, 0:4 * H])
+        wait("dve", "ld_a1", 16)
+        qa = quant(T.qa[:, H:NC], T.sa[:, H:NC], T.abf[:, 4 * H:2048])
+        need("gp", qa0)
+        send(relay_of[core], T.qa[:, 0:H], T.qa[:, 0:H], T.sa[:, 0:H], T.sa[:, 0:H], "rH")
         need("gp", qa)
-        for k in (1, 2, 3):
-            send(mate(k), T["la%d" % k][:], T.qa[:], T["las%d" % k][:], T.sa[:], "rA%d" % k)
-        sel, idn = quant_constants(*spread_diagonal(diag))
+        send_a(core, H, NC)
+        sel, idn = constants(diag)
         bq, bs = T.lb[:, 0:W], T.lbs[:, 0:W]
         src = helper_of[q] if q != rq else root
         wait("pe", "rB", 2 * engines(src, core))
         z = mm(0, bq, bs, T.qa[:], T.sa[:], NC, qa)
         terms.append((relu("act", T.r0[:], 0, 0, NC, z), T.r0))
         zbank = {1: 1, 2: 2, 3: 3}
+        lbank, vbank = (0, 4) if with_term else (4, 0)
 
-    for k in (1, 2, 3):
+    slots = [k for k in (1, 2, 3) if mate(-k) != root]
+
+    def landed(k):
         sender = mate(-k)
-        if sender == root:
-            continue
-        wait("pe", "rA%d" % k, 2 * engines(sender, core))
+        wait("pe", "rA%d" % k, 2 * engines(sender, core) + 2 * engines(relay_of[sender], core))
+
+    for n, k in enumerate(slots[:-1]):
+        landed(k)
         z = mm(zbank[k], bq, bs, T["la%d" % k][:], T["las%d" % k][:], NC)
-        buf = T["r%d" % k]
+        buf = T["r%d" % (n + 1)]
         terms.append((relu("act", buf[:], zbank[k], 0, NC, z), buf))
 
-    op, acc = terms[0]
-    last = len(terms) - (0 if with_term else 1)
-    for n in range(1, last):
-        out = (T.u1, T.u2)[n % 2]
-        op = add(out[:], acc[:], terms[n][1][:], op, terms[n][0])
-        acc = out
-    ops = []
+    op = two(T.u1[:], terms[0][1][:], terms[1][1][:], AluOpType.add, terms[0][0], terms[1][0])
     if with_term:
         wait("pe", "rT", 2 * engines(root, core))
         us = [mm(4 + i, T.qc[:, W * i:W * i + W], T.sc[:, W * i:W * i + W], T.lt[:, 0:W], T.lts[:, 0:W], W, sel)
               for i in range(4)]
         for i in range(4):
-            ops.append(add(T.p[:, i:NC:4], bank(4 + i, 0, W), acc[:, W * i:W * i + W], us[i], op, psum=4 + i))
+            op2 = two(T.acc[:, i:NC:4], bank(4 + i, 0, W), T.u1[:, W * i:W * i + W], AluOpType.add, us[i], op, psum=4 + i)
     else:
         for i in range(4):
-            ops.append(add(T.p[:, i:NC:4], acc[:, W * i:W * i + W], terms[-1][1][:, W * i:W * i + W], op, terms[-1][0]))
-    op = quant(T.qp[:], T.sp[:], T.p[:], ops[-1])
+            op2 = two(T.acc[:, i:NC:4], T.u1[:, W * i:W * i + W], terms[2][1][:, W * i:W * i + W], AluOpType.add,
+                      op, terms[2][0])
+    qs = quant(T.qs[:], T.ss[:], T.acc[:], op2)
+    for i in range(4):
+        mm(lbank + i, T.qc[:, W * i:W * i + W], T.sc[:, W * i:W * i + W], T.qs[:], T.ss[:], W, sel, qs, stop=False)
+    k = slots[-1]
+    landed(k)
+    zs = [mm(lbank + i, bq, bs, T["la%d" % k][:, W * i:W * i + W], T["las%d" % k][:, W * i:W * i + W], W, start=False)
+          for i in range(4)]
+    for i in range(4):
+        op = two(T.p[:, i:NC:4], bank(lbank + i, 0, W), T.acc[:, i:NC:4], AluOpType.max, zs[i], psum=lbank + i)
+    op = quant(T.qp[:], T.sp[:], T.p[:], op)
     need("gp", op)
     send(partner, T.lp[:, 0:W], T.qp[:, 0:W], T.lps[:, 0:W], T.sp[:, 0:W], "rP")
 
-    vb = 0 if is_root else 4
     wait("pe", "rP", 2 * engines(partner, core))
-    us = [mm(vb + i, T.qc[:, W * i:W * i + W], T.sc[:, W * i:W * i + W], T.lp[:, 0:W], T.lps[:, 0:W], W, sel)
+    us = [mm(vbank + i, T.qc[:, W * i:W * i + W], T.sc[:, W * i:W * i + W], T.lp[:, 0:W], T.lps[:, 0:W], W)
           for i in range(4)]
     for i in range(4):
-        op = add(T.tt[:, i:NC:4], bank(vb + i, 0, W), T.p[:, i:NC:4], us[i], psum=vb + i)
+        op = two(T.tt[:, i:NC:4], bank(vbank + i, 0, W), T.p[:, i:NC:4], AluOpType.add, us[i], psum=vbank + i)
     v = slice(W * q, W * q + W)
     tot = quant(T.gq[:, v], T.gs[:, v], T.tt[:], op)
     need("gp", tot)

from concourse.mybir import dt, AluOpType, ActivationFunctionType

W = 128
NC = 512
H = 192
CODE, BF, F32 = "float8_e4m3fn_x4", "bfloat16", "float32"

SCRATCH = {
    "abf": ("sbuf", [128, 2048], BF),
    "qa": ("sbuf", [128, NC], CODE), "sa": ("sbuf", [128, NC], "uint8"),
    "bbf": ("sbuf", [128, 2048], BF),
    "qb": ("sbuf", [128, NC], CODE), "sb": ("sbuf", [128, NC], "uint8"),
    "lb": ("sbuf", [128, W], CODE), "lbs": ("sbuf", [128, W], "uint8"),
    "la1": ("sbuf", [128, NC], CODE), "las1": ("sbuf", [128, NC], "uint8"),
    "la2": ("sbuf", [128, NC], CODE), "las2": ("sbuf", [128, NC], "uint8"),
    "la3": ("sbuf", [128, NC], CODE), "las3": ("sbuf", [128, NC], "uint8"),
    "t5": ("sbuf", [128, 2048], BF),
    "qt": ("sbuf", [128, NC], CODE), "st": ("sbuf", [128, NC], "uint8"),
    "lt": ("sbuf", [128, W], CODE), "lts": ("sbuf", [128, W], "uint8"),
    "ones": ("sbuf", [128, W], BF), "dg": ("sbuf", [128, W], BF),
    "cst": ("sbuf", [128, 4096], BF),
    "qc": ("sbuf", [128, 2 * NC], CODE), "sc": ("sbuf", [128, 2 * NC], "uint8"),
    "r0": ("sbuf", [128, NC], BF), "r1": ("sbuf", [128, NC], BF), "r2": ("sbuf", [128, NC], BF),
    "u1": ("sbuf", [128, NC], BF),
    "acc": ("sbuf", [128, NC], BF),
    "qs": ("sbuf", [128, W], CODE), "ss": ("sbuf", [128, W], "uint8"),
    "p": ("sbuf", [128, NC], BF),
    "qp": ("sbuf", [128, W], CODE), "sp": ("sbuf", [128, W], "uint8"),
    "lp": ("sbuf", [128, W], CODE), "lps": ("sbuf", [128, W], "uint8"),
    "tt": ("sbuf", [128, NC], BF),
    "gq": ("sbuf", [128, NC], CODE), "gs": ("sbuf", [128, NC], "uint8"),
    "ysb": ("sbuf", [128, 2048], F32),
    "ps": ("psum", [128, 4096], F32),
}
SEMAPHORES = ["ld_b0", "ld_b1", "ld_a0", "ld_a1", "yst", "pe", "act", "dve", "gp", "loc",
              "rH", "rB", "rA1", "rA2", "rA3", "rT", "rP", "rG1", "rG2", "rG3"]


def rank_program(g, core, T, topo):
    cores = T.cores
    root = cores[T.root]
    rank = T.rank_of(core)

    def far_cores(c):
        return [d for d in range(max(cores) + 8) if d < 256 and d not in cores and topo.host(d) == topo.host(c)
                and topo.chip(d) == topo.chip(c) and topo.die(d) != topo.die(c)]

    rq, rg = T.root // 2, T.root % 2
    foreign = [q for q in range(4) if q != rq]
    helper_of = {q: far_cores(root)[i] for i, q in enumerate(foreign)}
    relay_of = {c: far_cores(c)[0] for c in cores if c != root}

    sent = [0]

    def engines(src, dst):
        return bin(topo.mask(src, dst)).count("1")

    def send(dst, out_q, in_q, out_s, in_s, sem):
        rid, pid = topo.addr(dst, core)
        m = topo.mask(core, dst)
        g.remote_dma(out_q.bitcast(dt.uint8), in_q.bitcast(dt.uint8), T.sem[sem], T.sem.loc, pid, rid, m)
        g.remote_dma(out_s, in_s, T.sem[sem], T.sem.loc, pid, rid, m)
        sent[0] += 2 * engines(core, dst)

    def send_a(owner, lo, hi):
        r = T.rank_of(owner)
        for k in (1, 2, 3):
            send(cores[2 * ((r // 2 + k) % 4) + r % 2], T["la%d" % k][:, lo:hi], T.qa[:, lo:hi],
                 T["las%d" % k][:, lo:hi], T.sa[:, lo:hi], "rA%d" % k)

    if rank is None:
        for q in foreign:
            if helper_of[q] == core:
                g.wait_ge(T.sem.rB, 2 * engines(root, core))
                for grp in (rg, 1 - rg):
                    send(cores[2 * q + grp], T.lb[:, 0:W], T.lb[:, 0:W], T.lbs[:, 0:W], T.lbs[:, 0:W], "rB")
        for c in relay_of:
            if relay_of[c] == core:
                g.wait_ge(T.sem.rH, 2 * engines(c, core))
                send_a(c, 0, H)
        if sent[0]:
            g.wait_ge(T.sem.loc, sent[0])
        return

    q, grp = rank // 2, rank % 2
    is_root = core == root
    with_term = grp == rg and not is_root
    partner = cores[2 * q + 1 - grp]

    def mate(k):
        return cores[2 * ((q + k) % 4) + grp]

    eng = {"pe": g.tensor, "act": g.scalar, "dve": g.vector, "gp": g, "sync": g.sync}
    cnt = {"pe": 0, "act": 0, "dve": 0, "gp": 0}
    seen = {}

    def wait(queue, sem, n):
        if seen.get((queue, sem), 0) < n:
            seen[(queue, sem)] = n
            eng[queue].wait_ge(T.sem[sem], n)

    def did(queue, ins):
        cnt[queue] += 1
        ins.then_inc(T.sem[queue], 1)
        return (queue, cnt[queue])

    def need(queue, *ops):
        for op in ops:
            if op is not None:
                wait(queue, op[0], op[1])

    reader = {}

    def bank(b, lo=0, hi=NC):
        return T.ps[:, NC * b + lo:NC * b + hi]

    def mm(b, lq, ls, rq_, rs, n, *deps, start=True, stop=True):
        need("pe", *deps)
        need("pe", *reader.get(b, []))
        reader[b] = []
        return did("pe", g.tensor.matmul_mx(bank(b, 0, n), lq, ls, rq_, rs, start, stop))

    def relu(queue, out, b, lo, hi, *deps):
        need(queue, *deps)
        if queue == "act":
            op = did(queue, g.scalar.activation(out, bank(b, lo, hi), ActivationFunctionType.Relu))
        else:
            op = did(queue, g.vector.tensor_scalar(out, bank(b, lo, hi), 0.0, None, AluOpType.max))
        reader[b] = reader.get(b, []) + [op]
        return op

    def quant(oq, os, src, *deps):
        need("dve", *deps)
        return did("dve", g.vector.quantize_mx(oq, os, src))

    def two(out, a, b, alu, *deps, psum=None):
        need("dve", *deps)
        op = did("dve", g.vector.tensor_tensor(out, a, b, alu))
        if psum is not None:
            reader[psum] = reader.get(psum, []) + [op]
        return op

    if is_root:
        g.sync.dma_start(T.bbf[:, 0:1024], T.b[:, 0:1024]).then_inc(T.sem.ld_b0, 16)
        g.sync.dma_start(T.bbf[:, 1024:2048], T.b[:, 1024:2048]).then_inc(T.sem.ld_b1, 16)
        g.sync.wait_ge(T.sem.ld_b0, 16)
        g.sync.dma_start(T.abf[:], T.a[:]).then_inc(T.sem.ld_a0, 16)
    else:
        g.sync.dma_start(T.abf[:, 0:4 * H], T.a[:, 0:4 * H]).then_inc(T.sem.ld_a0, 16)
        g.sync.dma_start(T.abf[:, 4 * H:2048], T.a[:, 4 * H:2048]).then_inc(T.sem.ld_a1, 16)

    ones = did("dve", g.vector.memset(T.ones[:], 1.0))

    def make_diagonal():
        need("gp", ones)
        return did("gp", g.affine_select(T.dg[:], T.ones[:], [[-1, W]], AluOpType.is_equal, 0.0, 0, 1))

    def constants(diag):
        z0 = did("dve", g.vector.memset(T.cst[:, 0:2048], 0.0))
        z1 = did("dve", g.vector.memset(T.cst[:, 2048:4096], 0.0))
        cp = ActivationFunctionType.Copy
        need("act", diag, z0)
        for i in range(4):
            c0 = did("act", g.scalar.activation(T.cst[:, NC * i + i:NC * i + NC:4], T.dg[:], cp))
        need("act", z1)
        for t in range(4):
            c1 = did("act", g.scalar.activation(T.cst[:, 2048 + 5 * t:4096:16], T.dg[:], cp))
        s = quant(T.qc[:, 0:NC], T.sc[:, 0:NC], T.cst[:, 0:2048], c0)
        i = quant(T.qc[:, NC:2 * NC], T.sc[:, NC:2 * NC], T.cst[:, 2048:4096], c1)
        return s, i

    terms = []
    if is_root:
        wait("dve", "ld_b0", 16)
        h0 = quant(T.qb[:, 0:256], T.sb[:, 0:256], T.bbf[:, 0:1024])
        wait("dve", "ld_b1", 16)
        h1 = quant(T.qb[:, 256:512], T.sb[:, 256:512], T.bbf[:, 1024:2048])
        qb = {0: h0, 1: h0, 2: h1, 3: h1}
        wait("dve", "ld_a0", 16)
        qa = quant(T.qa[:], T.sa[:], T.abf[:])
        for f in foreign:
            need("gp", qb[f])
            v = slice(W * f, W * f + W)
            send(helper_of[f], T.lb[:, 0:W], T.qb[:, v], T.lbs[:, 0:W], T.sb[:, v], "rB")
        v = slice(W * q, W * q + W)
        need("gp", qb[q])
        send(partner, T.lb[:, 0:W], T.qb[:, v], T.lbs[:, 0:W], T.sb[:, v], "rB")
        diag = make_diagonal()
        order = [(q + k) % 4 for k in (1, 2, 3)]
        ready = {}
        for n, f in enumerate(order + [q]):
            v = slice(W * f, W * f + W)
            z = mm(n, T.qb[:, v], T.sb[:, v], T.qa[:], T.sa[:], NC, qb[f], qa)
            if f == q:
                terms.append((relu("act", T.r0[:], n, 0, NC, z), T.r0))
            else:
                on = "dve" if n == 1 else "act"
                ready[f] = [relu(on, T.t5[:, NC * f + i:NC * f + NC:4], n, W * i, W * i + W, z) for i in range(4)]
        for f in order:
            v = slice(W * f, W * f + W)
            op = quant(T.qt[:, v], T.st[:, v], T.t5[:, NC * f:NC * f + NC], *ready[f])
            need("gp", op)
            send(cores[2 * f + grp], T.lt[:, 0:W], T.qt[:, v], T.lts[:, 0:W], T.st[:, v], "rT")
        sel, idn = constants(diag)
        bq, bs = T.qb[:, W * q:W * q + W], T.sb[:, W * q:W * q + W]
        zbank, lbank, vbank = {1: 4, 2: 5, 3: 6}, 0, 4
    else:
        diag = make_diagonal()
        wait("dve", "ld_a0", 16)
        qa0 = quant(T.qa[:, 0:H], T.sa[:, 0:H], T.abf[:, 0:4 * H])
        wait("dve", "ld_a1", 16)
        qa = quant(T.qa[:, H:NC], T.sa[:, H:NC], T.abf[:, 4 * H:2048])
        need("gp", qa0)
        send(relay_of[core], T.qa[:, 0:H], T.qa[:, 0:H], T.sa[:, 0:H], T.sa[:, 0:H], "rH")
        need("gp", qa)
        send_a(core, H, NC)
        sel, idn = constants(diag)
        bq, bs = T.lb[:, 0:W], T.lbs[:, 0:W]
        src = helper_of[q] if q != rq else root
        wait("pe", "rB", 2 * engines(src, core))
        z = mm(0, bq, bs, T.qa[:], T.sa[:], NC, qa)
        terms.append((relu("act", T.r0[:], 0, 0, NC, z), T.r0))
        zbank = {1: 1, 2: 2, 3: 3}
        lbank, vbank = (0, 4) if with_term else (4, 0)

    slots = [k for k in (1, 2, 3) if mate(-k) != root]

    def landed(k):
        sender = mate(-k)
        wait("pe", "rA%d" % k, 2 * engines(sender, core) + 2 * engines(relay_of[sender], core))

    for n, k in enumerate(slots[:-1]):
        landed(k)
        z = mm(zbank[k], bq, bs, T["la%d" % k][:], T["las%d" % k][:], NC)
        buf = T["r%d" % (n + 1)]
        terms.append((relu("act", buf[:], zbank[k], 0, NC, z), buf))

    op = two(T.u1[:], terms[0][1][:], terms[1][1][:], AluOpType.add, terms[0][0], terms[1][0])
    if with_term:
        wait("pe", "rT", 2 * engines(root, core))
        us = [mm(4 + i, T.qc[:, W * i:W * i + W], T.sc[:, W * i:W * i + W], T.lt[:, 0:W], T.lts[:, 0:W], W, sel)
              for i in range(4)]
        for i in range(4):
            op2 = two(T.acc[:, i:NC:4], bank(4 + i, 0, W), T.u1[:, W * i:W * i + W], AluOpType.add, us[i], op, psum=4 + i)
    else:
        for i in range(4):
            op2 = two(T.acc[:, i:NC:4], T.u1[:, W * i:W * i + W], terms[2][1][:, W * i:W * i + W], AluOpType.add,
                      op, terms[2][0])
    qs = quant(T.qs[:], T.ss[:], T.acc[:], op2)
    for i in range(4):
        mm(lbank + i, T.qc[:, W * i:W * i + W], T.sc[:, W * i:W * i + W], T.qs[:], T.ss[:], W, sel, qs, stop=False)
    k = slots[-1]
    landed(k)
    zs = [mm(lbank + i, bq, bs, T["la%d" % k][:, W * i:W * i + W], T["las%d" % k][:, W * i:W * i + W], W, start=False)
          for i in range(4)]
    for i in range(4):
        op = two(T.p[:, i:NC:4], bank(lbank + i, 0, W), T.acc[:, i:NC:4], AluOpType.max, zs[i], psum=lbank + i)
    op = quant(T.qp[:], T.sp[:], T.p[:], op)
    need("gp", op)
    send(partner, T.lp[:, 0:W], T.qp[:, 0:W], T.lps[:, 0:W], T.sp[:, 0:W], "rP")

    wait("pe", "rP", 2 * engines(partner, core))
    us = [mm(vbank + i, T.qc[:, W * i:W * i + W], T.sc[:, W * i:W * i + W], T.lp[:, 0:W], T.lps[:, 0:W], W)
          for i in range(4)]
    for i in range(4):
        op = two(T.tt[:, i:NC:4], bank(vbank + i, 0, W), T.p[:, i:NC:4], AluOpType.add, us[i], psum=vbank + i)
    v = slice(W * q, W * q + W)
    tot = quant(T.gq[:, v], T.gs[:, v], T.tt[:], op)
    need("gp", tot)
    for k in (1, 2, 3):
        send(mate(k), T.gq[:, v], T.gq[:, v], T.gs[:, v], T.gs[:, v], "rG%d" % k)

    stored = 0
    for k in range(4):
        f = (q - k) % 4
        v = slice(W * f, W * f + W)
        if k:
            wait("pe", "rG%d" % k, 2 * engines(mate(-k), core))
        m = [mm(2 * k + h, T.gq[:, v], T.gs[:, v], T.qc[:, NC + 256 * h:NC + 256 * h + 256],
                T.sc[:, NC + 256 * h:NC + 256 * h + 256], 256, idn, tot) for h in range(2)]
        need("act", m[0])
        c0 = did("act", g.scalar.activation(T.ysb[:, NC * f:NC * f + 256], bank(2 * k, 0, 256), ActivationFunctionType.Copy))
        need("dve", m[1])
        c1 = did("dve", g.vector.tensor_copy(T.ysb[:, NC * f + 256:NC * f + NC], bank(2 * k + 1, 0, 256)))
        need("sync", c0, c1)
        g.sync.dma_start(T.y[:, NC * f:NC * f + NC], T.ysb[:, NC * f:NC * f + NC]).then_inc(T.sem.yst, 16)
        stored += 16
    g.sync.wait_ge(T.sem.yst, stored)
    g.wait_ge(T.sem.loc, sent[0])
    for name in ("pe", "act", "dve", "gp"):
        wait("sync", name, cnt[name])
